import numpy as np
import ml_dtypes


def mxq(x, axis, fmt="e4m3"):
    dtype, down = {"e4m3": (ml_dtypes.float8_e4m3fn, 7), "e5m2": (ml_dtypes.float8_e5m2, 14)}[fmt]
    v = np.moveaxis(np.asarray(x, np.float32).astype(ml_dtypes.bfloat16).astype(np.float64), axis, -1)
    blocks = v.reshape(v.shape[:-1] + (-1, 32))
    amax = np.abs(blocks).max(-1, keepdims=True)
    byte = np.maximum(np.where(amax > 0, np.frexp(amax)[1] - 1 + 127, 0) - down, 1)
    scale = np.exp2(byte - 127.0)
    codes = (blocks / scale).astype(np.float32).astype(dtype).astype(np.float64)
    return np.moveaxis((codes * scale).reshape(v.shape), -1, axis)


WIDE = False


def mx_kscale(k):
    if not WIDE:
        return np.ones(k)
    levels = np.array([10, -10, 5, -5, 0])
    if k % 512:
        return np.exp2(np.random.permutation(np.resize(levels, k // 32))).repeat(32)
    a = np.empty((k // 512, 16))
    for p in range(k // 512):
        a[p, :8] = np.random.permutation(np.resize(levels, 8))
        for g in range(8):
            far = levels[np.abs(levels - a[p, g]) >= 10]
            a[p, g + 8] = far[np.random.randint(len(far))]
    return np.exp2(a.ravel()).repeat(32)


BF16 = ml_dtypes.bfloat16


def bf(x):
    return np.asarray(x, np.float32).astype(BF16)


def f64(x):
    return np.asarray(x).astype(np.float64)


B, S, R, D, G = 2, 512, 4, 512, 16
C = D // G
K = 2 * R + R * R
RD = R * D
M = G * K
ROUNDS = 2


def sigmoid(v):
    return 1.0 / (1.0 + np.exp(-v))


def balance(l):
    q = np.exp(l)
    for _ in range(ROUNDS):
        q = q / np.sum(q, axis=-1, keepdims=True)
        q = q / np.sum(q, axis=-2, keepdims=True)
    return q


def read_streams(pre, xg):
    u = pre[..., 0][..., None] * xg[:, :, 0]
    for r in range(1, xg.shape[2]):
        u = u + pre[..., r][..., None] * xg[:, :, r]
    return u


def mix_streams(q, xg):
    qi = np.transpose(q, (0, 1, 3, 2, 4))
    y = qi[..., 0][..., None] * xg[:, :, 0][:, :, None]
    for j in range(1, xg.shape[2]):
        y = y + qi[..., j][..., None] * xg[:, :, j][:, :, None]
    return y


def draw0():
    s, t = mx_kscale(RD), mx_kscale(D)
    return {
        "x": bf(np.random.standard_normal((B, S, R, D))),
        "gn": bf((1.0 + 0.1 * np.random.standard_normal(RD)) * s),
        "phi": bf(1.5 * np.random.standard_normal((RD, M)) / np.sqrt(RD) / s[:, None]),
        "bm": bf(0.5 * np.random.standard_normal(M)),
        "gf": bf((1.0 + 0.1 * np.random.standard_normal(D)) * t),
        "w": bf(np.random.standard_normal((D, D)) / np.sqrt(D) / t[:, None]),
    }


def core(x, gn, phi, bm, gf, w):
    x = f64(x)
    b, s, r, d = x.shape

    xf = x.reshape(b, s, r * d)
    xn = xf * f64(gn)

    t = (mxq(xn, 2, "e4m3") @ mxq(f64(phi), 0, "e4m3")) + f64(bm)
    t = t.reshape(b, s, G, K)

    pre = sigmoid(t[..., 0:r])
    post = 2.0 * sigmoid(t[..., r:2 * r])
    l = t[..., 2 * r:].reshape(b, s, G, r, r)

    q = balance(l)

    xg = x.reshape(b, s, r, G, C)
    u = read_streams(pre, xg).reshape(b, s, d)

    ug = u * f64(gf)

    h = np.maximum(mxq(ug, 2, "e4m3") @ mxq(f64(w), 0, "e4m3"), 0.0)
    f = h * h
    fg = f.reshape(b, s, G, C)

    mixed = mix_streams(q, xg)
    post_i = np.transpose(post, (0, 1, 3, 2))
    y = mixed + post_i[..., None] * fg[:, :, None]
    return y.reshape(b, s, r, d)


def e4m3fn_bytes(y):
    return np.clip(np.asarray(y, np.float64), -448.0, 448.0).astype(np.float32).astype(ml_dtypes.float8_e4m3fn).view(np.uint8)


def e4m3fn_values(b):
    return np.asarray(b, np.uint8).view(ml_dtypes.float8_e4m3fn).astype(np.float64)


def setup_inputs():
    d = draw0()
    x0 = np.asarray(d['phi']).astype(np.float64)
    s = (np.max(np.abs(x0), axis=(1,), keepdims=True) / 448.0).astype(np.float32)
    out = {}
    for k, v in d.items():
        if k == 'phi':
            out['phi_bytes'] = e4m3fn_bytes(x0 / s.astype(np.float64))
            out['phi_scale'] = s
        else:
            out[k] = v
    return out


def reference(x, gn, phi_bytes, phi_scale, bm, gf, w):
    return core(x, gn, e4m3fn_values(phi_bytes) * phi_scale.astype(np.float64), bm, gf, w)

from contextlib import ExitStack

import concourse.mybir as mybir
from concourse.masks import make_identity

F32 = mybir.dt.float32
BF16 = mybir.dt.bfloat16
U32 = mybir.dt.uint32
U8 = mybir.dt.uint8
FP8 = mybir.dt.float8_e4m3fn
FP8X4 = mybir.dt.float8_e4m3fn_x4
ACT = mybir.ActivationFunctionType
ALU = mybir.AluOpType
AX = mybir.AxisListType

P = 128
T = 4
R = 4
D = 512
G = 16
C = 32
KC = 24
M = G * KC
TOK = 1024
NT = TOK // P
FLOPS = 2 * TOK * R * D * M + 2 * TOK * D * D

SCALAR_PAIRS = ((0, 2), (0, 3), (1, 2), (1, 3), (2, 2), (2, 3), (3, 2), (3, 3))


def spread(ap, axis, n):
    shape = list(ap.shape)
    shape.insert(axis, n)
    return ap.unsqueeze(axis).to_broadcast(shape)


def tile_groupedmanifoldhyperconnection_kernel(tc, x, gn, phi_bytes, phi_scale, bm, gf, w, out):
    nc = tc.nc
    x_rows = x.rearrange("b s r d -> (b s) (r d)")
    out_rows = out.rearrange("b s r d -> (b s) r d")
    with ExitStack() as ctx:
        keep = ctx.enter_context(tc.tile_pool(name="keep", bufs=1))
        sb = ctx.enter_context(tc.tile_pool(name="sb", bufs=2))
        ps = ctx.enter_context(tc.psum_pool(name="ps", bufs=1))

        ident = keep.tile([P, P], F32)
        make_identity(nc, ident[:])

        scale = keep.tile([P, R, T], F32)
        nc.sync.dma_start(out=scale[:], in_=phi_scale.rearrange("(r p t) o -> p r (t o)", p=P, t=T))
        phb = keep.tile([P, R, T, M], U8)
        phv = phi_bytes.rearrange("(r p t) n -> r p t n", p=P, t=T)
        for r in range(R):
            nc.sync.dma_start(out=phb[:, r, :, :], in_=phv[r])
        xs = []
        gns = keep.tile([P, R, T], BF16)
        gfs = keep.tile([P, T], BF16)
        bmz = keep.tile([P, M], BF16)
        wraw = keep.tile([P, T, D], BF16)
        nc.gpsimd.memset(bmz[:], 0.0)
        for n in range(NT):
            xt = keep.tile([P, R * D], BF16, name="x%d" % n)
            nc.sync.dma_start(out=xt[:], in_=x_rows[n * P : (n + 1) * P, :])
            xs.append(xt)
            if n == 0:
                nc.sync.dma_start(out=gns[:], in_=gn.rearrange("(r p t) -> p r t", p=P, t=T))
                nc.sync.dma_start(out=bmz[0:1, :], in_=bm.rearrange("(o n) -> o n", o=1))
            if n == 1:
                nc.sync.dma_start(out=wraw[:], in_=w.rearrange("(p t) n -> p t n", t=T))
                nc.sync.dma_start(out=gfs[:], in_=gf.rearrange("(p t) -> p t", t=T))

        sig = keep.tile([P, 2], F32)
        nc.gpsimd.memset(sig[0:64, :], 0.5)
        nc.gpsimd.memset(sig[64:128, :], 1.0)

        phc = keep.tile([P, R, M], U32, align_bytes=64)
        phs = keep.tile([P, R, M], U8, align_bytes=64)
        for r in range(R):
            phw = sb.tile([P, T, M], BF16, name="phw")
            for t in range(T):
                src = phb[:, r, t, :].bitcast(FP8)
                col = scale[:, r, t : t + 1]
                if t % 2 == 0:
                    nc.vector.tensor_scalar(phw[:, t, :], src, col, None, op0=ALU.mult)
                else:
                    nc.scalar.activation(phw[:, t, :], src, ACT.Copy, scale=col)
            phg = sb.tile([P, M, T], BF16, name="phg", align_bytes=64)
            nc.vector.tensor_copy(
                out=phg[:].rearrange("p (k g) t -> p k g t", g=G),
                in_=phw[:].rearrange("p t (g k) -> p k g t", g=G),
            )
            flat = phg[:].rearrange("p n t -> p (n t)")
            nc.vector.quantize_mx(out=phc[:, r, 0:128].bitcast(FP8X4), scales=phs[:, r, 0:128], in_=flat[:, 0:512])
            nc.vector.quantize_mx(out=phc[:, r, 128:384].bitcast(FP8X4), scales=phs[:, r, 128:384], in_=flat[:, 512:1536])

        bmp = keep.tile([P, M], F32)
        nc.scalar.copy(
            out=bmp[:].rearrange("p (k g) -> p k g", g=G), in_=bmz[:].rearrange("p (g k) -> p k g", g=G)
        )
        bps = ps.tile([P, 3, P], F32, name="ct")
        for m in range(3):
            nc.tensor.transpose(bps[:, m, :], bmp[:, m * P : (m + 1) * P], ident[:])
        bias = keep.tile([P, 3], F32)
        nc.vector.tensor_copy(out=bias[:], in_=bps[:, :, 0])
        hbias = keep.tile([P, 1], F32)
        nc.vector.tensor_scalar(hbias[:], bias[:, 0:1], 0.5, None, op0=ALU.mult)

        wg = keep.tile([P, D, T], BF16, align_bytes=64)
        nc.scalar.copy(out=wg[:], in_=wraw[:].rearrange("p t n -> p n t"))
        wc = keep.tile([P, D], U32, align_bytes=64)
        ws = keep.tile([P, D], U8, align_bytes=64)
        nc.vector.quantize_mx(out=wc[:].bitcast(FP8X4), scales=ws[:], in_=wg[:].rearrange("p n t -> p (n t)"))

        state = [dict() for n in range(NT)]

        def a_load(n, half):
            st = state[n]
            words = xs[n][:].bitcast(F32)
            if half == 0:
                st["xn"] = sb.tile([P, R, P, T], BF16, name="xn", align_bytes=64)
            xn = st["xn"]
            xp = ps.tile([P, 2, 2, P], F32, name="xp", bufs=2)
            for rr in range(2):
                r = 2 * half + rr
                for u in range(2):
                    nc.tensor.transpose(xp[:, rr, u, :], words[:, 256 * r + u : 256 * (r + 1) : 2], ident[:])
            for rr in range(2):
                r = 2 * half + rr
                nc.vector.tensor_tensor(
                    out=xn[:, r, :, :].rearrange("p k (u e) -> p k u e", e=2),
                    in0=xp[:, rr, :, :].rearrange("p u k -> p (u k)").bitcast(BF16).rearrange(
                        "p (u k e) -> p k u e", u=2, e=2
                    ),
                    in1=spread(gns[:, r, :].rearrange("p (u e) -> p u e", e=2), 1, P),
                    op=ALU.mult,
                )

        def a_quant(n):
            st = state[n]
            xqc = sb.tile([P, R, P], U32, name="xqc", align_bytes=64)
            xqs = sb.tile([P, R, P], U8, name="xqs", align_bytes=64)
            nc.vector.quantize_mx(
                out=xqc[:].rearrange("p r k -> p (r k)").bitcast(FP8X4),
                scales=xqs[:].rearrange("p r k -> p (r k)"),
                in_=st["xn"][:].rearrange("p r k t -> p (r k t)"),
            )
            st["xq"] = (xqc, xqs)

        def a_coef(n):
            st = state[n]
            xqc, xqs = st["xq"]
            tt = ps.tile([P, 3, P], F32, name="ct")
            for m in range(3):
                for r in range(R):
                    nc.tensor.matmul_mx(
                        out=tt[:, m, :],
                        lhsT=phc[:, r, m * P : (m + 1) * P].bitcast(FP8X4),
                        lhsT_scale=phs[:, r, m * P : (m + 1) * P],
                        rhs=xqc[:, r, :].bitcast(FP8X4),
                        rhs_scale=xqs[:, r, :],
                        start=(r == 0),
                        stop=(r == R - 1),
                    )
            co = sb.tile([P, 3, P], F32, name="co")
            for m in (1, 2):
                nc.scalar.activation(co[:, m, :], tt[:, m, :], ACT.Exp, bias=bias[:, m : m + 1])
            nc.scalar.activation(co[:, 0, :], tt[:, 0, :], ACT.Tanh, bias=hbias[:], scale=0.5)
            cs = sb.tile([P, P], F32, name="cs")
            nc.vector.tensor_scalar(cs[:], co[:, 0, :], sig[:, 0:1], sig[:, 1:2], op0=ALU.mult, op1=ALU.add)
            ee = ps.tile([P, 2, P], F32, name="ct")
            for m in (1, 2):
                nc.tensor.transpose(ee[:, m - 1, :], co[:, m, :], ident[:])
            st["cs"] = cs
            st["ee"] = ee

        def s_first(n):
            st = state[n]
            ev = st["ee"][:].rearrange("p a (b c g) -> p (a b) c g", b=2, g=G)
            q1 = sb.tile([P, R, R, G], F32, name="q1")
            s = sb.tile([P, R, G], F32, name="s1")
            v = sb.tile([P, R, G], F32, name="v1")
            nc.vector.tensor_reduce(s[:], ev.rearrange("p i j g -> p i g j"), axis=AX.X, op=ALU.add)
            nc.vector.reciprocal(v[:], s[:])
            nc.vector.tensor_tensor(out=q1[:], in0=ev, in1=spread(v[:], 2, R), op=ALU.mult)
            st["q"] = q1

        def s_step(n, step):
            st = state[n]
            cur = st["q"]
            s = sb.tile([P, R, G], F32, name="s%d" % (step + 2))
            v = sb.tile([P, R, G], F32, name="v%d" % (step + 2))
            nxt = sb.tile([P, R, R, G], F32, name="q%d" % (step + 2))
            order, axis = ("p i j g -> p j g i", 1) if step % 2 == 0 else ("p i j g -> p i g j", 2)
            nc.vector.tensor_reduce(s[:], cur[:].rearrange(order), axis=AX.X, op=ALU.add)
            nc.vector.reciprocal(v[:], s[:])
            nc.gpsimd.tensor_tensor(out=nxt[:], in0=cur[:], in1=spread(v[:], axis, R), op=ALU.mult)
            st["q"] = nxt

        def u_pp(n):
            st = state[n]
            pp = ps.tile([P, P], F32, name="pp")
            nc.tensor.transpose(pp[:], st["cs"][:], ident[:])
            st["pp"] = pp

        def u_prod(n):
            st = state[n]
            xt = xs[n]
            pp = st["pp"]
            up = []
            for r in range(R):
                pr = sb.tile([P, T, P], F32, name="pu", bufs=5)
                nc.vector.tensor_tensor(
                    out=pr[:].rearrange("p t (g c) -> p t g c", g=G),
                    in0=xt[:, r * D : (r + 1) * D].rearrange("p (g c t) -> p t g c", g=G, t=T),
                    in1=spread(spread(pp[:, r * G : (r + 1) * G], 2, 8), 1, T),
                    op=ALU.mult,
                )
                up.append(pr)
            ut = ps.tile([P, T, P], F32, name="uh")
            for t in range(T):
                for r in range(R):
                    nc.tensor.matmul(
                        ut[:, t, :], up[r][:, t, :], ident[:], start=(r == 0), stop=(r == R - 1), is_transpose=True
                    )
            st["ut"] = ut

        def u_quant(n):
            st = state[n]
            ug = sb.tile([P, P, T], BF16, name="ug", align_bytes=64)
            nc.vector.tensor_tensor(
                out=ug[:], in0=st["ut"][:].rearrange("p t k -> p k t"), in1=spread(gfs[:], 1, P), op=ALU.mult
            )
            ugc = sb.tile([P, P], U32, name="ugc", align_bytes=64)
            ugs = sb.tile([P, P], U8, name="ugs", align_bytes=64)
            nc.vector.quantize_mx(out=ugc[:].bitcast(FP8X4), scales=ugs[:], in_=ug[:].rearrange("p k t -> p (k t)"))
            st["ugq"] = (ugc, ugs)

        def u_h(n):
            st = state[n]
            ugc, ugs = st["ugq"]
            h = ps.tile([P, D], F32, name="uh")
            nc.tensor.matmul_mx(
                out=h[:], lhsT=ugc[:].bitcast(FP8X4), lhsT_scale=ugs[:], rhs=wc[:].bitcast(FP8X4), rhs_scale=ws[:],
                start=True, stop=True,
            )
            hr = sb.tile([P, D], F32, name="hr")
            nc.scalar.activation(hr[:], h[:], ACT.Relu)
            f = sb.tile([P, D], F32, name="f")
            nc.scalar.activation(f[:], hr[:], ACT.Square)
            st["f"] = f

        def u_f(n):
            st = state[n]
            pp = st["pp"]
            fi = []
            for i in range(R):
                pf = sb.tile([P, D], F32, name="pf", bufs=10)
                nc.vector.tensor_tensor(
                    out=pf[:].rearrange("p (g c) -> p g c", g=G),
                    in0=st["f"][:].rearrange("p (g c) -> p g c", g=G),
                    in1=spread(pp[:, (R + i) * G : (R + i + 1) * G], 2, C),
                    op=ALU.mult,
                )
                fi.append(pf)
            st["fi"] = fi

        def y_prod(n, i):
            st = state[n]
            xt = xs[n]
            q = st["q"]
            prods = []
            for j in range(R):
                pq = sb.tile([P, D], F32, name="pq", bufs=24)
                xj = xt[:, j * D : (j + 1) * D]
                if (i, j) in SCALAR_PAIRS:
                    for g in range(G):
                        nc.scalar.activation(
                            pq[:, g * C : (g + 1) * C], xj[:, g * C : (g + 1) * C], ACT.Copy, scale=q[:, i, j, g : g + 1]
                        )
                else:
                    nc.gpsimd.tensor_tensor(
                        out=pq[:].rearrange("p (g c) -> p g c", g=G),
                        in0=xj.rearrange("p (g c) -> p g c", g=G),
                        in1=spread(q[:, i, j, :], 2, C),
                        op=ALU.mult,
                    )
                prods.append(pq)
            st["prods%d" % i] = prods

        def y_out(n, i):
            st = state[n]
            prods = st["prods%d" % i]
            yt = ps.tile([P, 4, P], F32, name="yy", bufs=3)
            for b in range(4):
                for j in range(R):
                    nc.tensor.matmul(
                        yt[:, b, :], prods[j][:, b * P : (b + 1) * P], ident[:],
                        start=(j == 0), stop=(j == R - 1), is_transpose=True,
                    )
            ys = sb.tile([P, 4, P], F32, name="ys", bufs=3)
            nc.scalar.copy(out=ys[:], in_=yt[:])
            yb = ps.tile([P, 4, P], F32, name="yy", bufs=3)
            for b in range(4):
                nc.tensor.transpose(yb[:, b, :], ys[:, b, :], ident[:])
            yo = sb.tile([P, D], F32, name="yo", bufs=6)
            nc.vector.tensor_tensor(
                out=yo[:], in0=yb[:].rearrange("p b k -> p (b k)"), in1=st["fi"][i][:], op=ALU.add
            )
            nc.sync.dma_start(out=out_rows[n * P : (n + 1) * P, i, :], in_=yo[:])

        def do(fn, n, *args):
            if 0 <= n < NT:
                fn(n, *args)

        for k in range(-2, NT):
            if k >= 0:
                y_prod(k, 0)
            do(u_pp, k + 1)
            do(u_prod, k + 1)
            do(a_load, k + 2, 0)
            if k >= 0:
                y_prod(k, 1)
                y_out(k, 0)
            do(u_quant, k + 1)
            do(a_load, k + 2, 1)
            if k >= 0:
                y_prod(k, 2)
                y_out(k, 1)
            do(u_h, k + 1)
            do(a_quant, k + 2)
            do(a_coef, k + 2)
            do(s_first, k + 2)
            if k >= 0:
                y_prod(k, 3)
                y_out(k, 2)
            do(u_f, k + 1)
            for step in range(3):
                do(s_step, k + 2, step)
            if k >= 0:
                y_out(k, 3)
